import numpy as np, ml_dtypes
CORES = [32,160,288,416,80,208,336,464]
N = 8
NH, QP = 4, 64
def setup_inputs(rng):
    return {"q": rng.standard_normal((N, 128, NH * QP), dtype=np.float32).astype(ml_dtypes.bfloat16), "k": rng.standard_normal((N, 128, NH * 128), dtype=np.float32).astype(ml_dtypes.bfloat16), "v": rng.standard_normal((N, 128, NH * 128), dtype=np.float32).astype(ml_dtypes.bfloat16)}
def setup_inputs_big(rng):
    d = setup_inputs(rng)
    for k in ("q", "k", "v"): d[k] = (d[k].astype(np.float32) * 1024.0).astype(d[k].dtype)
    return d
def setup_inputs_small(rng):
    d = setup_inputs(rng)
    for k in ("q", "k", "v"): d[k] = (d[k].astype(np.float32) * (1 / 1024.0)).astype(d[k].dtype)
    return d
def setup_inputs_apart(rng):
    d = setup_inputs(rng)
    f = (10.0 ** rng.permutation(np.linspace(-1.5, 1.5, N))).astype(np.float32).reshape(N, 1, 1)
    for k in ("q", "k", "v"): d[k] = (d[k].astype(np.float32) * f).astype(d[k].dtype)
    return d
def reference(q, k, v):
    Q, K, V = q.astype(np.float64), k.astype(np.float64), v.astype(np.float64)
    y = np.zeros((N, 128, NH * QP))
    for r in range(N):
        for h in range(NH):
            for j in range(N):
                S = np.maximum(K[j][:, 128 * h:128 * h + 128].T @ Q[r][:, QP * h:QP * h + QP], 0.0)
                y[r][:, QP * h:QP * h + QP] += V[j][:, 128 * h:128 * h + 128].T @ S
    return {"y": y.astype(ml_dtypes.bfloat16 if q.dtype != np.float64 else np.float64)}

@@ -1,0 +1,127 @@
+from concourse.bass import DstId, RemoteDMATransfer
+from concourse.mybir import AluOpType
+
+NH, QP, KP = 4, 64, 128
+G = 4
+
+SCRATCH = {
+    "qall": ("sbuf", [128, G, NH, QP], "bfloat16"),
+    "kown": ("sbuf", [128, NH * KP], "bfloat16"),
+    "vown": ("sbuf", [128, NH * KP], "bfloat16"),
+    "kpar": ("sbuf", [128, NH * KP], "bfloat16"),
+    "vpar": ("sbuf", [128, NH * KP], "bfloat16"),
+    "zero": ("sbuf", [128, NH, QP], "float32"),
+    "s0": ("sbuf", [128, NH, G, QP], "bfloat16"),
+    "s1": ("sbuf", [128, NH, G, QP], "bfloat16"),
+    "osend": ("sbuf", [128, G - 1, NH, QP], "bfloat16"),
+    "orecv": ("sbuf", [128, G - 1, NH, QP], "bfloat16"),
+    "ysb": ("sbuf", [128, NH, QP], "bfloat16"),
+    "sps": ("psum", [128, G, 8, QP], "float32"),
+    "ops": ("psum", [128, NH, 8, QP], "float32"),
+}
+SEMAPHORES = (["ldq", "ldk", "ldv", "zs", "ka", "va0", "va1", "vs0", "vs1", "vo", "a1", "a2", "a3", "sent", "st"]
+              + ["qa%d" % x for x in range(G)] + ["oa%d" % d for d in range(1, G)]
+              + ["ts%d_%d" % (s, d) for s in range(2) for d in range(G)] + ["to%d" % h for h in range(NH)])
+
+
+def rank_program(g, core, T, topo):
+    if T.rank_of(core) is None:
+        return
+    sem, te, ve = T.sem, g.tensor, g.vector
+    rack = topo.rack(topo.host(core))
+    group = [c for c in T.cores if topo.rack(topo.host(c)) == rack]
+    partner = [c for c in T.cores if topo.rack(topo.host(c)) != rack and topo.may_write(core, c)
+               and topo.chip(c) == topo.chip(core)][0]
+    i = group.index(core)
+
+    def member(d):
+        return (i + d) % G
+
+    def engines(m):
+        return bin(m).count("1")
+
+    def head(t, h):
+        return t[:, h * KP:(h + 1) * KP]
+
+    g.sync.dma_start(T.qall[:, i], T.q[:]).then_inc(sem.ldq, 16)
+    g.scalar.dma_start(T.kown[:], T.k[:]).then_inc(sem.ldk, 16)
+    g.sync.dma_start(T.vown[:], T.v[:]).then_inc(sem.ldv, 16)
+    ve.memset(T.zero[:], 0.0).then_inc(sem.zs, 1)
+
+    sent = 0
+    peers = [group[member(d)] for d in range(1, G)]
+    mq = topo.mask(core, peers[0])
+    for p in peers:
+        mq &= topo.mask(core, p)
+    nq = engines(mq)
+    ids = [topo.addr(p, core) for p in peers]
+    g.wait_ge(sem.ldq, 16)
+    g.remote_dma_fused([RemoteDMATransfer(dst_ids=[DstId(rid=r, pnc=p) for r, p in ids], dma_engine_mask=mq,
+                                          remote_sem=sem["qa%d" % i], srcs=[T.qall[:, i]],
+                                          dsts=[T.qall[:, i] for _ in peers])], local_sem=sem.sent)
+    sent += nq
+    mp = topo.mask(core, partner)
+    np_ = engines(mp)
+    prid, ppid = topo.addr(partner, core)
+    g.wait_ge(sem.ldk, 16)
+    g.remote_dma(T.kpar[:], T.kown[:], sem.ka, sem.sent, ppid, prid, mp)
+    sent += np_
+    g.wait_ge(sem.ldv, 16)
+    half = NH * KP // 2
+    for b in range(2):
+        g.remote_dma(T.vpar[:, b * half:(b + 1) * half], T.vown[:, b * half:(b + 1) * half],
+                     sem["va%d" % b], sem.sent, ppid, prid, mp)
+        sent += np_
+    g.wait_ge(sem.vo, NH)
+    for d in range(1, G):
+        rid, pid = ids[d - 1]
+        g.remote_dma(T.orecv[:, d - 1], T.osend[:, d - 1], sem["oa%d" % d], sem.sent, pid, rid, mq)
+        sent += nq
+    g.wait_ge(sem.sent, sent)
+
+    order = [0] + list(range(G - 1, 0, -1))
+    te.wait_ge(sem.ldk, 16)
+    te.wait_ge(sem.ldq, 16)
+    for d in order:
+        if d:
+            te.wait_ge(sem["qa%d" % member(d)], nq)
+        for h in range(NH):
+            te.matmul(T.sps[:, d, h, :], head(T.kown, h), T.qall[:, member(d), h, :], True, True).then_inc(
+                sem["ts0_%d" % d], 1)
+    te.wait_ge(sem.ldv, 16)
+    te.wait_ge(sem.vs0, G)
+    for h in range(NH):
+        te.matmul(T.ops[:, h, 0:G, :], head(T.vown, h), T.s0[:, h], True, False)
+    te.wait_ge(sem.ka, np_)
+    for d in order:
+        for h in range(NH):
+            te.matmul(T.sps[:, d, h, :], head(T.kpar, h), T.qall[:, member(d), h, :], True, True).then_inc(
+                sem["ts1_%d" % d], 1)
+    te.wait_ge(sem.vs1, G)
+    for h in range(NH):
+        if h % 2 == 0:
+            te.wait_ge(sem["va%d" % (h // 2)], np_)
+        te.matmul(T.ops[:, h, 0:G, :], head(T.vpar, h), T.s1[:, h], False, True).then_inc(sem["to%d" % h], 1)
+
+    ve.wait_ge(sem.zs, 1)
+    for s, sb in ((0, T.s0), (1, T.s1)):
+        for d in order:
+            ve.wait_ge(sem["ts%d_%d" % (s, d)], NH)
+            ve.tensor_tensor(sb[:, :, d, :], T.sps[:, d, 0:NH, :], T.zero[:], AluOpType.max).then_inc(
+                sem["vs%d" % s], 1)
+    for h in range(NH):
+        ve.wait_ge(sem["to%d" % h], 1)
+        ve.tensor_copy(T.osend[:, :, h, :], T.ops[:, h, 1:G, :]).then_inc(sem.vo, 1)
+    ve.wait_ge(sem.vs1, G)
+    ve.wait_ge(sem.oa1, nq)
+    ve.tensor_tensor(T.sps[:, 0, 0:NH, :], T.ops[:, :, 0, :], T.orecv[:, 0], AluOpType.add).then_inc(sem.a1, 1)
+    ve.wait_ge(sem.a1, 1)
+    ve.wait_ge(sem.oa2, nq)
+    ve.tensor_tensor(T.sps[:, 1, 0:NH, :], T.sps[:, 0, 0:NH, :], T.orecv[:, 1], AluOpType.add).then_inc(sem.a2, 1)
+    ve.wait_ge(sem.a2, 1)
+    ve.wait_ge(sem.oa3, nq)
+    ve.tensor_tensor(T.ysb[:], T.sps[:, 1, 0:NH, :], T.orecv[:, 2], AluOpType.add).then_inc(sem.a3, 1)
+
+    g.sync.wait_ge(sem.a3, 1)
+    g.sync.dma_start(T.y[:], T.ysb[:]).then_inc(sem.st, 16)
+    g.sync.wait_ge(sem.st, 16)

@@ -19,9 +19,10 @@ SCRATCH = {
     "sps": ("psum", [128, G, 8, QP], "float32"),
     "ops": ("psum", [128, NH, 8, QP], "float32"),
 }
-SEMAPHORES = (["ldq", "ldk", "ldv", "zs", "ka", "va0", "va1", "vs0", "vs1", "vo", "a1", "a2", "a3", "sent", "st"]
+SEMAPHORES = (["ldq", "ldk", "ldv0", "ldv1", "zs", "ka0", "ka1", "va0", "va1", "vo", "a1", "a2", "a3", "sent", "st"]
               + ["qa%d" % x for x in range(G)] + ["oa%d" % d for d in range(1, G)]
-              + ["ts%d_%d" % (s, d) for s in range(2) for d in range(G)] + ["to%d" % h for h in range(NH)])
+              + ["ts%d_%d" % (s, d) for s in range(2) for d in range(G)] + ["to%d" % h for h in range(NH)]
+              + ["vp%d" % h for h in range(NH)] + ["vs%d" % d for d in range(G)])
 
 
 def rank_program(g, core, T, topo):
@@ -33,50 +34,60 @@ def rank_program(g, core, T, topo):
     partner = [c for c in T.cores if topo.rack(topo.host(c)) != rack and topo.may_write(core, c)
                and topo.chip(c) == topo.chip(core)][0]
     i = group.index(core)
+    half = NH * KP // 2
 
     def member(d):
         return (i + d) % G
 
-    def engines(m):
-        return bin(m).count("1")
-
     def head(t, h):
         return t[:, h * KP:(h + 1) * KP]
 
-    g.sync.dma_start(T.qall[:, i], T.q[:]).then_inc(sem.ldq, 16)
-    g.scalar.dma_start(T.kown[:], T.k[:]).then_inc(sem.ldk, 16)
-    g.sync.dma_start(T.vown[:], T.v[:]).then_inc(sem.ldv, 16)
+    def halfcols(t, b):
+        return t[:, b * half:(b + 1) * half]
+
+    def mask_of(bits):
+        return sum(1 << b for b in bits)
+
+    peers = [group[member(d)] for d in range(1, G)]
+    mall = topo.mask(core, partner)
+    for p in peers:
+        mall &= topo.mask(core, p)
+    bits = [b for b in range(16) if (mall >> b) & 1]
+    nall = len(bits)
+    qbits, rest = bits[0::2], bits[1::2]
+    kbits, vbits = rest[:len(rest) // 2], rest[len(rest) // 2:]
+    nq, nk, nv = len(qbits), len(kbits), len(vbits)
+
+    g.sync.dma_start(halfcols(T.vown, 1), halfcols(T.v, 1)).then_inc(sem.ldv1, 16)
+    g.scalar.dma_start(T.qall[:, i], T.q[:]).then_inc(sem.ldq, 16)
+    g.sync.dma_start(T.kown[:], T.k[:]).then_inc(sem.ldk, 16)
+    g.scalar.dma_start(halfcols(T.vown, 0), halfcols(T.v, 0)).then_inc(sem.ldv0, 16)
     ve.memset(T.zero[:], 0.0).then_inc(sem.zs, 1)
 
     sent = 0
-    peers = [group[member(d)] for d in range(1, G)]
-    mq = topo.mask(core, peers[0])
-    for p in peers:
-        mq &= topo.mask(core, p)
-    nq = engines(mq)
     ids = [topo.addr(p, core) for p in peers]
-    g.wait_ge(sem.ldq, 16)
-    g.remote_dma_fused([RemoteDMATransfer(dst_ids=[DstId(rid=r, pnc=p) for r, p in ids], dma_engine_mask=mq,
-                                          remote_sem=sem["qa%d" % i], srcs=[T.qall[:, i]],
-                                          dsts=[T.qall[:, i] for _ in peers])], local_sem=sem.sent)
-    sent += nq
-    mp = topo.mask(core, partner)
-    np_ = engines(mp)
     prid, ppid = topo.addr(partner, core)
+    g.wait_ge(sem.ldv1, 16)
+    g.remote_dma(halfcols(T.vpar, 1), halfcols(T.vown, 1), sem.va1, sem.sent, ppid, prid, mask_of(vbits))
+    sent += nv
+    g.wait_ge(sem.ldq, 16)
+    g.remote_dma_fused([RemoteDMATransfer(dst_ids=[DstId(rid=r, pnc=p) for r, p in ids],
+                                          dma_engine_mask=mask_of(qbits), remote_sem=sem["qa%d" % i],
+                                          srcs=[T.qall[:, i]], dsts=[T.qall[:, i] for _ in peers])],
+                       local_sem=sem.sent)
+    sent += nq
     g.wait_ge(sem.ldk, 16)
-    g.remote_dma(T.kpar[:], T.kown[:], sem.ka, sem.sent, ppid, prid, mp)
-    sent += np_
-    g.wait_ge(sem.ldv, 16)
-    half = NH * KP // 2
     for b in range(2):
-        g.remote_dma(T.vpar[:, b * half:(b + 1) * half], T.vown[:, b * half:(b + 1) * half],
-                     sem["va%d" % b], sem.sent, ppid, prid, mp)
-        sent += np_
+        g.remote_dma(halfcols(T.kpar, b), halfcols(T.kown, b), sem["ka%d" % b], sem.sent, ppid, prid, mask_of(kbits))
+        sent += nk
+    g.wait_ge(sem.ldv0, 16)
+    g.remote_dma(halfcols(T.vpar, 0), halfcols(T.vown, 0), sem.va0, sem.sent, ppid, prid, mask_of(qbits))
+    sent += nq
     g.wait_ge(sem.vo, NH)
     for d in range(1, G):
         rid, pid = ids[d - 1]
-        g.remote_dma(T.orecv[:, d - 1], T.osend[:, d - 1], sem["oa%d" % d], sem.sent, pid, rid, mq)
-        sent += nq
+        g.remote_dma(T.orecv[:, d - 1], T.osend[:, d - 1], sem["oa%d" % d], sem.sent, pid, rid, mall)
+        sent += nall
     g.wait_ge(sem.sent, sent)
 
     order = [0] + list(range(G - 1, 0, -1))
@@ -88,38 +99,52 @@ def rank_program(g, core, T, topo):
         for h in range(NH):
             te.matmul(T.sps[:, d, h, :], head(T.kown, h), T.qall[:, member(d), h, :], True, True).then_inc(
                 sem["ts0_%d" % d], 1)
-    te.wait_ge(sem.ldv, 16)
-    te.wait_ge(sem.vs0, G)
+
+    def partner_scores(h):
+        te.wait_ge(sem["vs%d" % order[h]], 1)
+        for d in order:
+            te.matmul(T.sps[:, order[h], d, :], head(T.kpar, h), T.qall[:, member(d), h, :], True, True).then_inc(
+                sem["ts1_%d" % h], 1)
+
+    te.wait_ge(sem.ka0, nk)
+    partner_scores(0)
+    partner_scores(1)
+    te.wait_ge(sem.ldv0, 16)
+    te.wait_ge(sem.ldv1, 16)
+    for d in order:
+        te.wait_ge(sem["vs%d" % d], 1)
     for h in range(NH):
         te.matmul(T.ops[:, h, 0:G, :], head(T.vown, h), T.s0[:, h], True, False)
-    te.wait_ge(sem.ka, np_)
-    for d in order:
-        for h in range(NH):
-            te.matmul(T.sps[:, d, h, :], head(T.kpar, h), T.qall[:, member(d), h, :], True, True).then_inc(
-                sem["ts1_%d" % d], 1)
-    te.wait_ge(sem.vs1, G)
+    te.wait_ge(sem.ka1, nk)
+    partner_scores(2)
+    partner_scores(3)
     for h in range(NH):
         if h % 2 == 0:
-            te.wait_ge(sem["va%d" % (h // 2)], np_)
+            te.wait_ge(sem["va%d" % (h // 2)], (nq, nv)[h // 2])
+        te.wait_ge(sem["vp%d" % h], 1)
         te.matmul(T.ops[:, h, 0:G, :], head(T.vpar, h), T.s1[:, h], False, True).then_inc(sem["to%d" % h], 1)
 
     ve.wait_ge(sem.zs, 1)
-    for s, sb in ((0, T.s0), (1, T.s1)):
-        for d in order:
-            ve.wait_ge(sem["ts%d_%d" % (s, d)], NH)
-            ve.tensor_tensor(sb[:, :, d, :], T.sps[:, d, 0:NH, :], T.zero[:], AluOpType.max).then_inc(
-                sem["vs%d" % s], 1)
+    for d in order:
+        ve.wait_ge(sem["ts0_%d" % d], NH)
+        ve.tensor_tensor(T.s0[:, :, d, :], T.sps[:, d, 0:NH, :], T.zero[:], AluOpType.max).then_inc(
+            sem["vs%d" % d], 1)
+    for h in range(NH):
+        ve.wait_ge(sem["ts1_%d" % h], G)
+        ve.tensor_tensor(T.s1[:, h], T.sps[:, order[h], 0:G, :], T.zero[:], AluOpType.max).then_inc(
+            sem["vp%d" % h], 1)
     for h in range(NH):
         ve.wait_ge(sem["to%d" % h], 1)
         ve.tensor_copy(T.osend[:, :, h, :], T.ops[:, h, 1:G, :]).then_inc(sem.vo, 1)
-    ve.wait_ge(sem.vs1, G)
-    ve.wait_ge(sem.oa1, nq)
+    for h in range(NH):
+        ve.wait_ge(sem["vp%d" % h], 1)
+    ve.wait_ge(sem.oa1, nall)
     ve.tensor_tensor(T.sps[:, 0, 0:NH, :], T.ops[:, :, 0, :], T.orecv[:, 0], AluOpType.add).then_inc(sem.a1, 1)
     ve.wait_ge(sem.a1, 1)
-    ve.wait_ge(sem.oa2, nq)
+    ve.wait_ge(sem.oa2, nall)
     ve.tensor_tensor(T.sps[:, 1, 0:NH, :], T.sps[:, 0, 0:NH, :], T.orecv[:, 1], AluOpType.add).then_inc(sem.a2, 1)
     ve.wait_ge(sem.a2, 1)
-    ve.wait_ge(sem.oa3, nq)
+    ve.wait_ge(sem.oa3, nall)
     ve.tensor_tensor(T.ysb[:], T.sps[:, 1, 0:NH, :], T.orecv[:, 2], AluOpType.add).then_inc(sem.a3, 1)
 
     g.sync.wait_ge(sem.a3, 1)

@@ -1,8 +1,12 @@
 from concourse.bass import DstId, RemoteDMATransfer
-from concourse.mybir import AluOpType
+from concourse.mybir import AluOpType, ActivationFunctionType
 
 NH, QP, KP = 4, 64, 128
 G = 4
+NG = 2 * G
+NB = 4
+SPLIT = [(0, 2), (2, 3), (3, 4)]
+NW = len(SPLIT)
 
 SCRATCH = {
     "qall": ("sbuf", [128, G, NH, QP], "bfloat16"),
@@ -13,139 +17,199 @@ SCRATCH = {
     "zero": ("sbuf", [128, NH, QP], "float32"),
     "s0": ("sbuf", [128, NH, G, QP], "bfloat16"),
     "s1": ("sbuf", [128, NH, G, QP], "bfloat16"),
-    "osend": ("sbuf", [128, G - 1, NH, QP], "bfloat16"),
-    "orecv": ("sbuf", [128, G - 1, NH, QP], "bfloat16"),
+    "osend": ("sbuf", [128, G, NH, QP], "bfloat16"),
+    "orecv": ("sbuf", [128, G, NH, QP], "bfloat16"),
     "ysb": ("sbuf", [128, NH, QP], "bfloat16"),
-    "sps": ("psum", [128, G, 8, QP], "float32"),
+    "sps": ("psum", [128, NB, 8, QP], "float32"),
     "ops": ("psum", [128, NH, 8, QP], "float32"),
 }
-SEMAPHORES = (["ldq", "ldk", "ldv0", "ldv1", "zs", "ka0", "ka1", "va0", "va1", "vo", "a1", "a2", "a3", "sent", "st"]
-              + ["qa%d" % x for x in range(G)] + ["oa%d" % d for d in range(1, G)]
-              + ["ts%d_%d" % (s, d) for s in range(2) for d in range(G)] + ["to%d" % h for h in range(NH)]
-              + ["vp%d" % h for h in range(NH)] + ["vs%d" % d for d in range(G)])
+SEMAPHORES = (["inq", "ink", "inv", "zs", "ka", "va", "vo", "a1a", "a1b", "a2", "a3", "sent", "st"]
+              + ["qa%d" % t for t in range(1, G)] + ["oa%d_%d" % (w, t) for w in range(NW) for t in range(G)]
+              + ["ts%d" % n for n in range(NG)] + ["rl%d" % n for n in range(NG)] + ["to%d" % h for h in range(NH)])
 
 
 def rank_program(g, core, T, topo):
-    if T.rank_of(core) is None:
-        return
-    sem, te, ve = T.sem, g.tensor, g.vector
-    rack = topo.rack(topo.host(core))
-    group = [c for c in T.cores if topo.rack(topo.host(c)) == rack]
-    partner = [c for c in T.cores if topo.rack(topo.host(c)) != rack and topo.may_write(core, c)
-               and topo.chip(c) == topo.chip(core)][0]
-    i = group.index(core)
-    half = NH * KP // 2
+    def on_chip(a, b):
+        return topo.host(a) == topo.host(b) and topo.chip(a) == topo.chip(b)
 
-    def member(d):
-        return (i + d) % G
+    def workers(r):
+        base = r - r % topo.CORES_PER_CHIP
+        chipc = [c for c in range(base, base + topo.CORES_PER_CHIP) if c != r]
+        same = [c for c in chipc if topo.die(c) == topo.die(r)]
+        other = [c for c in chipc if topo.die(c) != topo.die(r)]
+        return [r, same[-1], other[-1]]
+
+    home = [r for r in T.cores if on_chip(r, core)]
+    if not home or core not in workers(home[0]):
+        return
+    home = home[0]
+    w = workers(home).index(core)
+    h0, h1 = SPLIT[w]
+    nh = h1 - h0
+
+    sem, te, ve, ac = T.sem, g.tensor, g.vector, g.scalar
+    rack = topo.rack(topo.host(home))
+    group = [c for c in T.cores if topo.rack(topo.host(c)) == rack]
+    partner = [c for c in T.cores if topo.rack(topo.host(c)) != rack and topo.may_write(home, c)
+               and topo.chip(c) == topo.chip(home)][0]
+    i = group.index(home)
 
     def head(t, h):
         return t[:, h * KP:(h + 1) * KP]
 
-    def halfcols(t, b):
-        return t[:, b * half:(b + 1) * half]
+    def heads(t, a, b):
+        return t[:, a * KP:b * KP]
 
     def mask_of(bits):
         return sum(1 << b for b in bits)
 
-    peers = [group[member(d)] for d in range(1, G)]
-    mall = topo.mask(core, partner)
-    for p in peers:
-        mall &= topo.mask(core, p)
-    bits = [b for b in range(16) if (mall >> b) & 1]
+    def bits_of(m):
+        return [b for b in range(16) if (m >> b) & 1]
+
+    mall = topo.mask(core, workers(partner)[w])
+    for p in group:
+        if p != home:
+            mall &= topo.mask(core, workers(p)[w]) & topo.mask(core, p)
+    bits = bits_of(mall)
     nall = len(bits)
-    qbits, rest = bits[0::2], bits[1::2]
-    kbits, vbits = rest[:len(rest) // 2], rest[len(rest) // 2:]
-    nq, nk, nv = len(qbits), len(kbits), len(vbits)
+    qbits, kbits = bits[0::2], bits[1::2]
+    nq, nk = len(qbits), len(kbits)
+    mq, mk = mask_of(qbits), mask_of(kbits)
 
-    g.sync.dma_start(halfcols(T.vown, 1), halfcols(T.v, 1)).then_inc(sem.ldv1, 16)
-    g.scalar.dma_start(T.qall[:, i], T.q[:]).then_inc(sem.ldq, 16)
-    g.sync.dma_start(T.kown[:], T.k[:]).then_inc(sem.ldk, 16)
-    g.scalar.dma_start(halfcols(T.vown, 0), halfcols(T.v, 0)).then_inc(sem.ldv0, 16)
+    def push_bits(x):
+        free = [b for b in bits_of(topo.mask(home, workers(home)[x])) if b not in bits]
+        n = len(free) // (NW - 1)
+        return free[(x - 1) * n:x * n]
+
+    nin = 16 if w == 0 else len(push_bits(w))
+
     ve.memset(T.zero[:], 0.0).then_inc(sem.zs, 1)
+    if w == 0:
+        ac.dma_start(T.qall[:, 0], T.q[:]).then_inc(sem.inq, 16)
+        g.sync.dma_start(T.kown[:], T.k[:]).then_inc(sem.ink, 16)
+        ac.dma_start(T.vown[:], T.v[:]).then_inc(sem.inv, 16)
 
-    sent = 0
-    ids = [topo.addr(p, core) for p in peers]
-    prid, ppid = topo.addr(partner, core)
-    g.wait_ge(sem.ldv1, 16)
-    g.remote_dma(halfcols(T.vpar, 1), halfcols(T.vown, 1), sem.va1, sem.sent, ppid, prid, mask_of(vbits))
-    sent += nv
-    g.wait_ge(sem.ldq, 16)
-    g.remote_dma_fused([RemoteDMATransfer(dst_ids=[DstId(rid=r, pnc=p) for r, p in ids],
-                                          dma_engine_mask=mask_of(qbits), remote_sem=sem["qa%d" % i],
-                                          srcs=[T.qall[:, i]], dsts=[T.qall[:, i] for _ in peers])],
-                       local_sem=sem.sent)
-    sent += nq
-    g.wait_ge(sem.ldk, 16)
-    for b in range(2):
-        g.remote_dma(halfcols(T.kpar, b), halfcols(T.kown, b), sem["ka%d" % b], sem.sent, ppid, prid, mask_of(kbits))
-        sent += nk
-    g.wait_ge(sem.ldv0, 16)
-    g.remote_dma(halfcols(T.vpar, 0), halfcols(T.vown, 0), sem.va0, sem.sent, ppid, prid, mask_of(qbits))
-    sent += nq
-    g.wait_ge(sem.vo, NH)
-    for d in range(1, G):
-        rid, pid = ids[d - 1]
-        g.remote_dma(T.orecv[:, d - 1], T.osend[:, d - 1], sem["oa%d" % d], sem.sent, pid, rid, mall)
-        sent += nall
-    g.wait_ge(sem.sent, sent)
+    sent = [0]
 
-    order = [0] + list(range(G - 1, 0, -1))
-    te.wait_ge(sem.ldk, 16)
-    te.wait_ge(sem.ldq, 16)
-    for d in order:
-        if d:
-            te.wait_ge(sem["qa%d" % member(d)], nq)
-        for h in range(NH):
-            te.matmul(T.sps[:, d, h, :], head(T.kown, h), T.qall[:, member(d), h, :], True, True).then_inc(
-                sem["ts0_%d" % d], 1)
+    def push(dst_of):
+        if w:
+            return
+        for x in range(1, NW):
+            a, b = SPLIT[x]
+            ap, s = dst_of(a, b)
+            rid, pid = topo.addr(workers(home)[x], core)
+            g.remote_dma(ap, ap, s, sem.sent, pid, rid, mask_of(push_bits(x)))
+            sent[0] += len(push_bits(x))
 
-    def partner_scores(h):
-        te.wait_ge(sem["vs%d" % order[h]], 1)
-        for d in order:
-            te.matmul(T.sps[:, order[h], d, :], head(T.kpar, h), T.qall[:, member(d), h, :], True, True).then_inc(
-                sem["ts1_%d" % h], 1)
+    prid, ppid = topo.addr(workers(partner)[w], core)
+    g.wait_ge(sem.inq, nin)
+    push(lambda a, b: (T.qall[:, 0, a:b, :], sem.inq))
+    for t in range(1, G):
+        rid, pid = topo.addr(workers(group[(i + t) % G])[w], core)
+        g.remote_dma(T.qall[:, t, h0:h1, :], T.qall[:, 0, h0:h1, :], sem["qa%d" % t], sem.sent, pid, rid, mq)
+        sent[0] += nq
+    g.wait_ge(sem.ink, nin)
+    push(lambda a, b: (heads(T.kown, a, b), sem.ink))
+    g.remote_dma(heads(T.kpar, h0, h1), heads(T.kown, h0, h1), sem.ka, sem.sent, ppid, prid, mk)
+    sent[0] += nk
+    g.wait_ge(sem.inv, nin)
+    push(lambda a, b: (heads(T.vown, a, b), sem.inv))
+    g.remote_dma(heads(T.vpar, h0, h1), heads(T.vown, h0, h1), sem.va, sem.sent, ppid, prid, mk)
+    sent[0] += nk
+    g.wait_ge(sem.vo, nh)
+    for t in list(range(1, G)) + ([0] if w else []):
+        rid, pid = topo.addr(group[(i - t) % G], core)
+        g.remote_dma(T.orecv[:, t, h0:h1, :], T.osend[:, t, h0:h1, :], sem["oa%d_%d" % (w, t)], sem.sent,
+                     pid, rid, mall)
+        sent[0] += nall
+    g.wait_ge(sem.sent, sent[0])
 
-    te.wait_ge(sem.ka0, nk)
-    partner_scores(0)
-    partner_scores(1)
-    te.wait_ge(sem.ldv0, 16)
-    te.wait_ge(sem.ldv1, 16)
-    for d in order:
-        te.wait_ge(sem["vs%d" % d], 1)
-    for h in range(NH):
-        te.matmul(T.ops[:, h, 0:G, :], head(T.vown, h), T.s0[:, h], True, False)
-    te.wait_ge(sem.ka1, nk)
-    partner_scores(2)
-    partner_scores(3)
-    for h in range(NH):
-        if h % 2 == 0:
-            te.wait_ge(sem["va%d" % (h // 2)], (nq, nv)[h // 2])
-        te.wait_ge(sem["vp%d" % h], 1)
-        te.matmul(T.ops[:, h, 0:G, :], head(T.vpar, h), T.s1[:, h], False, True).then_inc(sem["to%d" % h], 1)
+    groups = [(0, 0), (0, 1), (0, 2), (1, 0), (1, 1), (1, 2), (0, 3), (1, 3)]
+    early = G - 1
+
+    def scores(n):
+        kind, p = groups[n]
+        if n >= NB:
+            te.wait_ge(sem["rl%d" % (n - NB)], 1)
+        kk = (T.kown, T.kpar)[kind]
+        for h in range(h0, h1):
+            te.matmul(T.sps[:, n % NB, h - h0, :], head(kk, h), T.qall[:, p, h, :], True, True).then_inc(
+                sem["ts%d" % n], 1)
+
+    te.wait_ge(sem.ink, nin)
+    te.wait_ge(sem.inq, nin)
+    scores(0)
+    te.wait_ge(sem.qa1, nq)
+    scores(1)
+    te.wait_ge(sem.qa2, nq)
+    scores(2)
+    te.wait_ge(sem.inv, nin)
+    for n in range(3):
+        te.wait_ge(sem["rl%d" % n], 1)
+    for h in range(h0, h1):
+        te.matmul(T.ops[:, h - h0, 0:early, :], head(T.vown, h), T.s0[:, h, 0:early, :], True, False)
+    te.wait_ge(sem.ka, nk)
+    scores(3)
+    scores(4)
+    scores(5)
+    te.wait_ge(sem.qa3, nq)
+    scores(6)
+    scores(7)
+    for n in range(3, NG):
+        te.wait_ge(sem["rl%d" % n], 1)
+    te.wait_ge(sem.va, nk)
+    for h in range(h0, h1):
+        te.matmul(T.ops[:, h - h0, 0:early, :], head(T.vpar, h), T.s1[:, h, 0:early, :], False, True).then_inc(
+            sem["to%d" % h], 1)
+        te.matmul(T.ops[:, h - h0, early, :], head(T.vown, h), T.s0[:, h, early, :], True, False)
+        te.matmul(T.ops[:, h - h0, early, :], head(T.vpar, h), T.s1[:, h, early, :], False, True).then_inc(
+            sem["to%d" % h], 1)
 
     ve.wait_ge(sem.zs, 1)
-    for d in order:
-        ve.wait_ge(sem["ts0_%d" % d], NH)
-        ve.tensor_tensor(T.s0[:, :, d, :], T.sps[:, d, 0:NH, :], T.zero[:], AluOpType.max).then_inc(
-            sem["vs%d" % d], 1)
-    for h in range(NH):
-        ve.wait_ge(sem["ts1_%d" % h], G)
-        ve.tensor_tensor(T.s1[:, h], T.sps[:, order[h], 0:G, :], T.zero[:], AluOpType.max).then_inc(
-            sem["vp%d" % h], 1)
-    for h in range(NH):
-        ve.wait_ge(sem["to%d" % h], 1)
-        ve.tensor_copy(T.osend[:, :, h, :], T.ops[:, h, 1:G, :]).then_inc(sem.vo, 1)
-    for h in range(NH):
-        ve.wait_ge(sem["vp%d" % h], 1)
-    ve.wait_ge(sem.oa1, nall)
-    ve.tensor_tensor(T.sps[:, 0, 0:NH, :], T.ops[:, :, 0, :], T.orecv[:, 0], AluOpType.add).then_inc(sem.a1, 1)
-    ve.wait_ge(sem.a1, 1)
-    ve.wait_ge(sem.oa2, nall)
-    ve.tensor_tensor(T.sps[:, 1, 0:NH, :], T.sps[:, 0, 0:NH, :], T.orecv[:, 1], AluOpType.add).then_inc(sem.a2, 1)
+    for n in range(NG):
+        kind, p = groups[n]
+        out = (T.s0, T.s1)[kind][:, h0:h1, p, :]
+        if n % 2 == 0:
+            ve.wait_ge(sem["ts%d" % n], nh)
+            ve.tensor_tensor(out, T.sps[:, n % NB, 0:nh, :], T.zero[:, 0:nh, :], AluOpType.max).then_inc(
+                sem["rl%d" % n], 1)
+        else:
+            ac.wait_ge(sem["ts%d" % n], nh)
+            ac.activation(out, T.sps[:, n % NB, 0:nh, :], ActivationFunctionType.Relu).then_inc(sem["rl%d" % n], 1)
+    first = 0 if w else 1
+    for h in range(h0, h1):
+        if (h - h0) % 2 == 0:
+            ve.wait_ge(sem["to%d" % h], 2)
+            ve.tensor_copy(T.osend[:, first:G, h, :], T.ops[:, h - h0, first:G, :]).then_inc(sem.vo, 1)
+        else:
+            ac.wait_ge(sem["to%d" % h], 2)
+            ac.activation(T.osend[:, first:G, h, :], T.ops[:, h - h0, first:G, :],
+                          ActivationFunctionType.Copy).then_inc(sem.vo, 1)
+    if w:
+        return
+
+    def arrived(t, ws):
+        for x in ws:
+            ve.wait_ge(sem["oa%d_%d" % (x, t)], nall)
+
+    helpers = list(range(1, NW))
+    ve.wait_ge(sem.vo, nh)
+    for n in range(NG):
+        ve.wait_ge(sem["rl%d" % n], 1)
+    arrived(1, [0])
+    ve.tensor_tensor(T.sps[:, 0, 0:h1, :], T.ops[:, 0:nh, 0, :], T.orecv[:, 1, 0:h1, :], AluOpType.add).then_inc(
+        sem.a1a, 1)
+    arrived(0, helpers)
+    arrived(1, helpers)
+    ve.tensor_tensor(T.sps[:, 0, h1:NH, :], T.orecv[:, 0, h1:NH, :], T.orecv[:, 1, h1:NH, :], AluOpType.add).then_inc(
+        sem.a1b, 1)
+    ve.wait_ge(sem.a1a, 1)
+    ve.wait_ge(sem.a1b, 1)
+    arrived(2, range(NW))
+    ve.tensor_tensor(T.sps[:, 1, 0:NH, :], T.sps[:, 0, 0:NH, :], T.orecv[:, 2], AluOpType.add).then_inc(sem.a2, 1)
     ve.wait_ge(sem.a2, 1)
-    ve.wait_ge(sem.oa3, nall)
-    ve.tensor_tensor(T.ysb[:], T.sps[:, 1, 0:NH, :], T.orecv[:, 2], AluOpType.add).then_inc(sem.a3, 1)
+    arrived(3, range(NW))
+    ve.tensor_tensor(T.ysb[:], T.sps[:, 1, 0:NH, :], T.orecv[:, 3], AluOpType.add).then_inc(sem.a3, 1)
 
     g.sync.wait_ge(sem.a3, 1)
     g.sync.dma_start(T.y[:], T.ysb[:]).then_inc(sem.st, 16)

@@ -5,8 +5,8 @@ NH, QP, KP = 4, 64, 128
 G = 4
 NG = 2 * G
 NB = 4
-SPLIT = [(0, 2), (2, 3), (3, 4)]
-NW = len(SPLIT)
+NW = NH
+TS = 2
 
 SCRATCH = {
     "qall": ("sbuf", [128, G, NH, QP], "bfloat16"),
@@ -14,18 +14,21 @@ SCRATCH = {
     "vown": ("sbuf", [128, NH * KP], "bfloat16"),
     "kpar": ("sbuf", [128, NH * KP], "bfloat16"),
     "vpar": ("sbuf", [128, NH * KP], "bfloat16"),
-    "zero": ("sbuf", [128, NH, QP], "float32"),
-    "s0": ("sbuf", [128, NH, G, QP], "bfloat16"),
-    "s1": ("sbuf", [128, NH, G, QP], "bfloat16"),
+    "zero": ("sbuf", [128, QP], "float32"),
+    "ones": ("sbuf", [128, 128], "bfloat16"),
+    "ident": ("sbuf", [128, 128], "bfloat16"),
+    "s0": ("sbuf", [128, G, QP], "bfloat16"),
+    "s1": ("sbuf", [128, G, QP], "bfloat16"),
     "osend": ("sbuf", [128, G, NH, QP], "bfloat16"),
     "orecv": ("sbuf", [128, G, NH, QP], "bfloat16"),
     "ysb": ("sbuf", [128, NH, QP], "bfloat16"),
     "sps": ("psum", [128, NB, 8, QP], "float32"),
-    "ops": ("psum", [128, NH, 8, QP], "float32"),
+    "ops": ("psum", [128, G, 8, QP], "float32"),
 }
-SEMAPHORES = (["inq", "ink", "inv", "zs", "ka", "va", "vo", "a1a", "a1b", "a2", "a3", "sent", "st"]
+SEMAPHORES = (["inq", "ink", "inv", "zs", "ons", "idn", "ka", "va", "a1b", "a2b", "a3", "sent", "st"]
               + ["qa%d" % t for t in range(1, G)] + ["oa%d_%d" % (w, t) for w in range(NW) for t in range(G)]
-              + ["ts%d" % n for n in range(NG)] + ["rl%d" % n for n in range(NG)] + ["to%d" % h for h in range(NH)])
+              + ["ts%d" % n for n in range(NG)] + ["rl%d" % n for n in range(NG)]
+              + ["to%d" % p for p in range(G)] + ["vo%d" % p for p in range(G)] + ["zt%d" % x for x in range(TS)])
 
 
 def rank_program(g, core, T, topo):
@@ -37,15 +40,14 @@ def rank_program(g, core, T, topo):
         chipc = [c for c in range(base, base + topo.CORES_PER_CHIP) if c != r]
         same = [c for c in chipc if topo.die(c) == topo.die(r)]
         other = [c for c in chipc if topo.die(c) != topo.die(r)]
-        return [r, same[-1], other[-1]]
+        return [r, same[-1], other[0], other[-1]]
 
     home = [r for r in T.cores if on_chip(r, core)]
     if not home or core not in workers(home[0]):
         return
     home = home[0]
     w = workers(home).index(core)
-    h0, h1 = SPLIT[w]
-    nh = h1 - h0
+    h = w
 
     sem, te, ve, ac = T.sem, g.tensor, g.vector, g.scalar
     rack = topo.rack(topo.host(home))
@@ -54,11 +56,8 @@ def rank_program(g, core, T, topo):
                and topo.chip(c) == topo.chip(home)][0]
     i = group.index(home)
 
-    def head(t, h):
-        return t[:, h * KP:(h + 1) * KP]
-
-    def heads(t, a, b):
-        return t[:, a * KP:b * KP]
+    def head(t, x):
+        return t[:, x * KP:(x + 1) * KP]
 
     def mask_of(bits):
         return sum(1 << b for b in bits)
@@ -77,9 +76,12 @@ def rank_program(g, core, T, topo):
     mq, mk = mask_of(qbits), mask_of(kbits)
 
     def push_bits(x):
-        free = [b for b in bits_of(topo.mask(home, workers(home)[x])) if b not in bits]
-        n = len(free) // (NW - 1)
-        return free[(x - 1) * n:x * n]
+        return [b for b in bits_of(topo.mask(home, workers(home)[x])) if b not in bits]
+
+    def home_bits(x):
+        hc = workers(home)[x]
+        off = topo.mask(hc, workers(partner)[x])
+        return [b for b in bits_of(topo.mask(hc, home)) if not (off >> b) & 1][0::2]
 
     nin = 16 if w == 0 else len(push_bits(w))
 
@@ -88,6 +90,9 @@ def rank_program(g, core, T, topo):
         ac.dma_start(T.qall[:, 0], T.q[:]).then_inc(sem.inq, 16)
         g.sync.dma_start(T.kown[:], T.k[:]).then_inc(sem.ink, 16)
         ac.dma_start(T.vown[:], T.v[:]).then_inc(sem.inv, 16)
+        ve.memset(T.ones[:], 1.0).then_inc(sem.ons, 1)
+        g.wait_ge(sem.ons, 1)
+        g.affine_select(T.ident[:], T.ones[:], [[-1, 128]], AluOpType.is_equal, 0.0, 0, 1).then_inc(sem.idn, 1)
 
     sent = [0]
 
@@ -95,46 +100,51 @@ def rank_program(g, core, T, topo):
         if w:
             return
         for x in range(1, NW):
-            a, b = SPLIT[x]
-            ap, s = dst_of(a, b)
+            ap, s = dst_of(x)
             rid, pid = topo.addr(workers(home)[x], core)
             g.remote_dma(ap, ap, s, sem.sent, pid, rid, mask_of(push_bits(x)))
             sent[0] += len(push_bits(x))
 
     prid, ppid = topo.addr(workers(partner)[w], core)
     g.wait_ge(sem.inq, nin)
-    push(lambda a, b: (T.qall[:, 0, a:b, :], sem.inq))
+    push(lambda x: (T.qall[:, 0, x, :], sem.inq))
     for t in range(1, G):
         rid, pid = topo.addr(workers(group[(i + t) % G])[w], core)
-        g.remote_dma(T.qall[:, t, h0:h1, :], T.qall[:, 0, h0:h1, :], sem["qa%d" % t], sem.sent, pid, rid, mq)
+        g.remote_dma(T.qall[:, t, h, :], T.qall[:, 0, h, :], sem["qa%d" % t], sem.sent, pid, rid, mq)
         sent[0] += nq
     g.wait_ge(sem.ink, nin)
-    push(lambda a, b: (heads(T.kown, a, b), sem.ink))
-    g.remote_dma(heads(T.kpar, h0, h1), heads(T.kown, h0, h1), sem.ka, sem.sent, ppid, prid, mk)
+    push(lambda x: (head(T.kown, x), sem.ink))
+    g.remote_dma(head(T.kpar, h), head(T.kown, h), sem.ka, sem.sent, ppid, prid, mk)
     sent[0] += nk
     g.wait_ge(sem.inv, nin)
-    push(lambda a, b: (heads(T.vown, a, b), sem.inv))
-    g.remote_dma(heads(T.vpar, h0, h1), heads(T.vown, h0, h1), sem.va, sem.sent, ppid, prid, mk)
+    push(lambda x: (head(T.vown, x), sem.inv))
+    g.remote_dma(head(T.vpar, h), head(T.vown, h), sem.va, sem.sent, ppid, prid, mk)
     sent[0] += nk
-    g.wait_ge(sem.vo, nh)
-    for t in list(range(1, G)) + ([0] if w else []):
+    if w:
+        g.wait_ge(sem.vo0, 1)
+        rid, pid = topo.addr(home, core)
+        g.remote_dma(T.orecv[:, 0, h, :], T.osend[:, 0, h, :], sem["oa%d_0" % w], sem.sent,
+                     pid, rid, mask_of(home_bits(w)))
+        sent[0] += len(home_bits(w))
+    for t in range(1, G):
+        g.wait_ge(sem["vo%d" % t], 1)
         rid, pid = topo.addr(group[(i - t) % G], core)
-        g.remote_dma(T.orecv[:, t, h0:h1, :], T.osend[:, t, h0:h1, :], sem["oa%d_%d" % (w, t)], sem.sent,
-                     pid, rid, mall)
+        g.remote_dma(T.orecv[:, t, h, :], T.osend[:, t, h, :], sem["oa%d_%d" % (w, t)], sem.sent, pid, rid, mall)
         sent[0] += nall
     g.wait_ge(sem.sent, sent[0])
 
     groups = [(0, 0), (0, 1), (0, 2), (1, 0), (1, 1), (1, 2), (0, 3), (1, 3)]
-    early = G - 1
 
     def scores(n):
         kind, p = groups[n]
         if n >= NB:
             te.wait_ge(sem["rl%d" % (n - NB)], 1)
         kk = (T.kown, T.kpar)[kind]
-        for h in range(h0, h1):
-            te.matmul(T.sps[:, n % NB, h - h0, :], head(kk, h), T.qall[:, p, h, :], True, True).then_inc(
-                sem["ts%d" % n], 1)
+        te.matmul(T.sps[:, n % NB, 0, :], head(kk, h), T.qall[:, p, h, :], True, True).then_inc(sem["ts%d" % n], 1)
+
+    def own_half(p):
+        te.wait_ge(sem["rl%d" % groups.index((0, p))], 1)
+        te.matmul(T.ops[:, p, 0, :], head(T.vown, h), T.s0[:, p, :], True, False)
 
     te.wait_ge(sem.ink, nin)
     te.wait_ge(sem.inq, nin)
@@ -144,10 +154,8 @@ def rank_program(g, core, T, topo):
     te.wait_ge(sem.qa2, nq)
     scores(2)
     te.wait_ge(sem.inv, nin)
-    for n in range(3):
-        te.wait_ge(sem["rl%d" % n], 1)
-    for h in range(h0, h1):
-        te.matmul(T.ops[:, h - h0, 0:early, :], head(T.vown, h), T.s0[:, h, 0:early, :], True, False)
+    for p in range(G - 1):
+        own_half(p)
     te.wait_ge(sem.ka, nk)
     scores(3)
     scores(4)
@@ -155,62 +163,71 @@ def rank_program(g, core, T, topo):
     te.wait_ge(sem.qa3, nq)
     scores(6)
     scores(7)
-    for n in range(3, NG):
-        te.wait_ge(sem["rl%d" % n], 1)
+    own_half(G - 1)
     te.wait_ge(sem.va, nk)
-    for h in range(h0, h1):
-        te.matmul(T.ops[:, h - h0, 0:early, :], head(T.vpar, h), T.s1[:, h, 0:early, :], False, True).then_inc(
-            sem["to%d" % h], 1)
-        te.matmul(T.ops[:, h - h0, early, :], head(T.vown, h), T.s0[:, h, early, :], True, False)
-        te.matmul(T.ops[:, h - h0, early, :], head(T.vpar, h), T.s1[:, h, early, :], False, True).then_inc(
-            sem["to%d" % h], 1)
+    for p in list(range(1, G)) + [0] if w == 0 else range(G):
+        te.wait_ge(sem["rl%d" % groups.index((1, p))], 1)
+        if w == 0 and p == 0:
+            te.matmul(T.ops[:, p, 0, :], head(T.vpar, h), T.s1[:, p, :], False, False)
+        else:
+            te.matmul(T.ops[:, p, 0, :], head(T.vpar, h), T.s1[:, p, :], False, True).then_inc(sem["to%d" % p], 1)
 
     ve.wait_ge(sem.zs, 1)
     for n in range(NG):
         kind, p = groups[n]
-        out = (T.s0, T.s1)[kind][:, h0:h1, p, :]
+        out = (T.s0, T.s1)[kind][:, p, :]
         if n % 2 == 0:
-            ve.wait_ge(sem["ts%d" % n], nh)
-            ve.tensor_tensor(out, T.sps[:, n % NB, 0:nh, :], T.zero[:, 0:nh, :], AluOpType.max).then_inc(
-                sem["rl%d" % n], 1)
+            ve.wait_ge(sem["ts%d" % n], 1)
+            ve.tensor_tensor(out, T.sps[:, n % NB, 0, :], T.zero[:], AluOpType.max).then_inc(sem["rl%d" % n], 1)
         else:
-            ac.wait_ge(sem["ts%d" % n], nh)
-            ac.activation(out, T.sps[:, n % NB, 0:nh, :], ActivationFunctionType.Relu).then_inc(sem["rl%d" % n], 1)
-    first = 0 if w else 1
-    for h in range(h0, h1):
-        if (h - h0) % 2 == 0:
-            ve.wait_ge(sem["to%d" % h], 2)
-            ve.tensor_copy(T.osend[:, first:G, h, :], T.ops[:, h - h0, first:G, :]).then_inc(sem.vo, 1)
+            ac.wait_ge(sem["ts%d" % n], 1)
+            ac.activation(out, T.sps[:, n % NB, 0, :], ActivationFunctionType.Relu).then_inc(sem["rl%d" % n], 1)
+    for p in range(0 if w else 1, G):
+        if p % 2 == 0:
+            ve.wait_ge(sem["to%d" % p], 1)
+            ve.tensor_copy(T.osend[:, p, h, :], T.ops[:, p, 0, :]).then_inc(sem["vo%d" % p], 1)
         else:
-            ac.wait_ge(sem["to%d" % h], 2)
-            ac.activation(T.osend[:, first:G, h, :], T.ops[:, h - h0, first:G, :],
-                          ActivationFunctionType.Copy).then_inc(sem.vo, 1)
+            ac.wait_ge(sem["to%d" % p], 1)
+            ac.activation(T.osend[:, p, h, :], T.ops[:, p, 0, :], ActivationFunctionType.Copy).then_inc(
+                sem["vo%d" % p], 1)
     if w:
         return
 
-    def arrived(t, ws):
+    def arrived(q, t, ws):
         for x in ws:
-            ve.wait_ge(sem["oa%d_%d" % (x, t)], nall)
+            q.wait_ge(sem["oa%d_%d" % (x, t)], nall if t else len(home_bits(x)))
 
-    helpers = list(range(1, NW))
-    ve.wait_ge(sem.vo, nh)
+    acc = [T.ops[:, 0, 0, :]] + [T.sps[:, x - 1, 0, :] for x in range(1, TS)]
+    te.wait_ge(sem.idn, 1)
+    for step, t in enumerate([1, 2, 0, 3]):
+        for x in range(TS):
+            if x == 0 and t == 0:
+                continue
+            arrived(te, t, [x])
+            mm = te.matmul(acc[x], T.ident[:], T.orecv[:, t, x, :], x > 0 and step == 0, t == 3)
+            if t == 3:
+                mm.then_inc(sem["zt%d" % x], 1)
+    for x in range(TS):
+        ac.wait_ge(sem["zt%d" % x], 1)
+        ac.activation(T.ysb[:, x, :], acc[x], ActivationFunctionType.Copy).then_inc(sem.a3, 1)
+
+    vh = list(range(TS, NW))
+    b1, b2 = NB - 2, NB - 1
     for n in range(NG):
         ve.wait_ge(sem["rl%d" % n], 1)
-    arrived(1, [0])
-    ve.tensor_tensor(T.sps[:, 0, 0:h1, :], T.ops[:, 0:nh, 0, :], T.orecv[:, 1, 0:h1, :], AluOpType.add).then_inc(
-        sem.a1a, 1)
-    arrived(0, helpers)
-    arrived(1, helpers)
-    ve.tensor_tensor(T.sps[:, 0, h1:NH, :], T.orecv[:, 0, h1:NH, :], T.orecv[:, 1, h1:NH, :], AluOpType.add).then_inc(
+    arrived(ve, 1, vh)
+    arrived(ve, 2, vh)
+    ve.tensor_tensor(T.sps[:, b1, TS:NH, :], T.orecv[:, 1, TS:NH, :], T.orecv[:, 2, TS:NH, :], AluOpType.add).then_inc(
         sem.a1b, 1)
-    ve.wait_ge(sem.a1a, 1)
     ve.wait_ge(sem.a1b, 1)
-    arrived(2, range(NW))
-    ve.tensor_tensor(T.sps[:, 1, 0:NH, :], T.sps[:, 0, 0:NH, :], T.orecv[:, 2], AluOpType.add).then_inc(sem.a2, 1)
-    ve.wait_ge(sem.a2, 1)
-    arrived(3, range(NW))
-    ve.tensor_tensor(T.ysb[:], T.sps[:, 1, 0:NH, :], T.orecv[:, 3], AluOpType.add).then_inc(sem.a3, 1)
+    arrived(ve, 0, vh)
+    ve.tensor_tensor(T.sps[:, b2, TS:NH, :], T.sps[:, b1, TS:NH, :], T.orecv[:, 0, TS:NH, :], AluOpType.add).then_inc(
+        sem.a2b, 1)
+    ve.wait_ge(sem.a2b, 1)
+    arrived(ve, 3, vh)
+    ve.tensor_tensor(T.ysb[:, TS:NH, :], T.sps[:, b2, TS:NH, :], T.orecv[:, 3, TS:NH, :], AluOpType.add).then_inc(
+        sem.a3, 1)
 
-    g.sync.wait_ge(sem.a3, 1)
+    g.sync.wait_ge(sem.a3, TS + 1)
     g.sync.dma_start(T.y[:], T.ysb[:]).then_inc(sem.st, 16)
     g.sync.wait_ge(sem.st, 16)

from concourse.bass import DstId, RemoteDMATransfer
from concourse.mybir import AluOpType, ActivationFunctionType

NH, QP, KP = 4, 64, 128
G = 4
NG = 2 * G
NB = 4
NW = NH
TS = 2

SCRATCH = {
    "qall": ("sbuf", [128, G, NH, QP], "bfloat16"),
    "kown": ("sbuf", [128, NH * KP], "bfloat16"),
    "vown": ("sbuf", [128, NH * KP], "bfloat16"),
    "kpar": ("sbuf", [128, NH * KP], "bfloat16"),
    "vpar": ("sbuf", [128, NH * KP], "bfloat16"),
    "zero": ("sbuf", [128, QP], "float32"),
    "ones": ("sbuf", [128, 128], "bfloat16"),
    "ident": ("sbuf", [128, 128], "bfloat16"),
    "s0": ("sbuf", [128, G, QP], "bfloat16"),
    "s1": ("sbuf", [128, G, QP], "bfloat16"),
    "osend": ("sbuf", [128, G, NH, QP], "bfloat16"),
    "orecv": ("sbuf", [128, G, NH, QP], "bfloat16"),
    "ysb": ("sbuf", [128, NH, QP], "bfloat16"),
    "sps": ("psum", [128, NB, 8, QP], "float32"),
    "ops": ("psum", [128, G, 8, QP], "float32"),
}
SEMAPHORES = (["inq", "ink", "inv", "zs", "ons", "idn", "ka", "va", "a1b", "a2b", "a3", "sent", "st"]
              + ["qa%d" % t for t in range(1, G)] + ["oa%d_%d" % (w, t) for w in range(NW) for t in range(G)]
              + ["ts%d" % n for n in range(NG)] + ["rl%d" % n for n in range(NG)]
              + ["to%d" % p for p in range(G)] + ["vo%d" % p for p in range(G)] + ["zt%d" % x for x in range(TS)])


def rank_program(g, core, T, topo):
    def on_chip(a, b):
        return topo.host(a) == topo.host(b) and topo.chip(a) == topo.chip(b)

    def workers(r):
        base = r - r % topo.CORES_PER_CHIP
        chipc = [c for c in range(base, base + topo.CORES_PER_CHIP) if c != r]
        same = [c for c in chipc if topo.die(c) == topo.die(r)]
        other = [c for c in chipc if topo.die(c) != topo.die(r)]
        return [r, same[-1], other[0], other[-1]]

    home = [r for r in T.cores if on_chip(r, core)]
    if not home or core not in workers(home[0]):
        return
    home = home[0]
    w = workers(home).index(core)
    h = w

    sem, te, ve, ac = T.sem, g.tensor, g.vector, g.scalar
    rack = topo.rack(topo.host(home))
    group = [c for c in T.cores if topo.rack(topo.host(c)) == rack]
    partner = [c for c in T.cores if topo.rack(topo.host(c)) != rack and topo.may_write(home, c)
               and topo.chip(c) == topo.chip(home)][0]
    i = group.index(home)

    def head(t, x):
        return t[:, x * KP:(x + 1) * KP]

    def mask_of(bits):
        return sum(1 << b for b in bits)

    def bits_of(m):
        return [b for b in range(16) if (m >> b) & 1]

    mall = topo.mask(core, workers(partner)[w])
    for p in group:
        if p != home:
            mall &= topo.mask(core, workers(p)[w]) & topo.mask(core, p)
    bits = bits_of(mall)
    nall = len(bits)
    qbits, kbits = bits[0::2], bits[1::2]
    nq, nk = len(qbits), len(kbits)
    mq, mk = mask_of(qbits), mask_of(kbits)

    def push_bits(x):
        return [b for b in bits_of(topo.mask(home, workers(home)[x])) if b not in bits]

    def home_bits(x):
        hc = workers(home)[x]
        off = topo.mask(hc, workers(partner)[x])
        return [b for b in bits_of(topo.mask(hc, home)) if not (off >> b) & 1][0::2]

    nin = 16 if w == 0 else len(push_bits(w))

    ve.memset(T.zero[:], 0.0).then_inc(sem.zs, 1)
    if w == 0:
        ac.dma_start(T.qall[:, 0], T.q[:]).then_inc(sem.inq, 16)
        g.sync.dma_start(T.kown[:], T.k[:]).then_inc(sem.ink, 16)
        ac.dma_start(T.vown[:], T.v[:]).then_inc(sem.inv, 16)
        ve.memset(T.ones[:], 1.0).then_inc(sem.ons, 1)
        g.wait_ge(sem.ons, 1)
        g.affine_select(T.ident[:], T.ones[:], [[-1, 128]], AluOpType.is_equal, 0.0, 0, 1).then_inc(sem.idn, 1)

    sent = [0]

    def push(dst_of):
        if w:
            return
        for x in range(1, NW):
            ap, s = dst_of(x)
            rid, pid = topo.addr(workers(home)[x], core)
            g.remote_dma(ap, ap, s, sem.sent, pid, rid, mask_of(push_bits(x)))
            sent[0] += len(push_bits(x))

    prid, ppid = topo.addr(workers(partner)[w], core)
    g.wait_ge(sem.inq, nin)
    push(lambda x: (T.qall[:, 0, x, :], sem.inq))
    for t in range(1, G):
        rid, pid = topo.addr(workers(group[(i + t) % G])[w], core)
        g.remote_dma(T.qall[:, t, h, :], T.qall[:, 0, h, :], sem["qa%d" % t], sem.sent, pid, rid, mq)
        sent[0] += nq
    g.wait_ge(sem.ink, nin)
    push(lambda x: (head(T.kown, x), sem.ink))
    g.remote_dma(head(T.kpar, h), head(T.kown, h), sem.ka, sem.sent, ppid, prid, mk)
    sent[0] += nk
    g.wait_ge(sem.inv, nin)
    push(lambda x: (head(T.vown, x), sem.inv))
    g.remote_dma(head(T.vpar, h), head(T.vown, h), sem.va, sem.sent, ppid, prid, mk)
    sent[0] += nk
    if w:
        g.wait_ge(sem.vo0, 1)
        rid, pid = topo.addr(home, core)
        g.remote_dma(T.orecv[:, 0, h, :], T.osend[:, 0, h, :], sem["oa%d_0" % w], sem.sent,
                     pid, rid, mask_of(home_bits(w)))
        sent[0] += len(home_bits(w))
    for t in range(1, G):
        g.wait_ge(sem["vo%d" % t], 1)
        rid, pid = topo.addr(group[(i - t) % G], core)
        g.remote_dma(T.orecv[:, t, h, :], T.osend[:, t, h, :], sem["oa%d_%d" % (w, t)], sem.sent, pid, rid, mall)
        sent[0] += nall
    g.wait_ge(sem.sent, sent[0])

    groups = [(0, 0), (0, 1), (0, 2), (1, 0), (1, 1), (1, 2), (0, 3), (1, 3)]

    def scores(n):
        kind, p = groups[n]
        if n >= NB:
            te.wait_ge(sem["rl%d" % (n - NB)], 1)
        kk = (T.kown, T.kpar)[kind]
        te.matmul(T.sps[:, n % NB, 0, :], head(kk, h), T.qall[:, p, h, :], True, True).then_inc(sem["ts%d" % n], 1)

    def own_half(p):
        te.wait_ge(sem["rl%d" % groups.index((0, p))], 1)
        te.matmul(T.ops[:, p, 0, :], head(T.vown, h), T.s0[:, p, :], True, False)

    te.wait_ge(sem.ink, nin)
    te.wait_ge(sem.inq, nin)
    scores(0)
    te.wait_ge(sem.qa1, nq)
    scores(1)
    te.wait_ge(sem.qa2, nq)
    scores(2)
    te.wait_ge(sem.inv, nin)
    for p in range(G - 1):
        own_half(p)
    te.wait_ge(sem.ka, nk)
    scores(3)
    scores(4)
    scores(5)
    te.wait_ge(sem.qa3, nq)
    scores(6)
    scores(7)
    own_half(G - 1)
    te.wait_ge(sem.va, nk)
    for p in list(range(1, G)) + [0] if w == 0 else range(G):
        te.wait_ge(sem["rl%d" % groups.index((1, p))], 1)
        if w == 0 and p == 0:
            te.matmul(T.ops[:, p, 0, :], head(T.vpar, h), T.s1[:, p, :], False, False)
        else:
            te.matmul(T.ops[:, p, 0, :], head(T.vpar, h), T.s1[:, p, :], False, True).then_inc(sem["to%d" % p], 1)

    ve.wait_ge(sem.zs, 1)
    for n in range(NG):
        kind, p = groups[n]
        out = (T.s0, T.s1)[kind][:, p, :]
        if n % 2 == 0:
            ve.wait_ge(sem["ts%d" % n], 1)
            ve.tensor_tensor(out, T.sps[:, n % NB, 0, :], T.zero[:], AluOpType.max).then_inc(sem["rl%d" % n], 1)
        else:
            ac.wait_ge(sem["ts%d" % n], 1)
            ac.activation(out, T.sps[:, n % NB, 0, :], ActivationFunctionType.Relu).then_inc(sem["rl%d" % n], 1)
    for p in range(0 if w else 1, G):
        if p % 2 == 0:
            ve.wait_ge(sem["to%d" % p], 1)
            ve.tensor_copy(T.osend[:, p, h, :], T.ops[:, p, 0, :]).then_inc(sem["vo%d" % p], 1)
        else:
            ac.wait_ge(sem["to%d" % p], 1)
            ac.activation(T.osend[:, p, h, :], T.ops[:, p, 0, :], ActivationFunctionType.Copy).then_inc(
                sem["vo%d" % p], 1)
    if w:
        return

    def arrived(q, t, ws):
        for x in ws:
            q.wait_ge(sem["oa%d_%d" % (x, t)], nall if t else len(home_bits(x)))

    acc = [T.ops[:, 0, 0, :]] + [T.sps[:, x - 1, 0, :] for x in range(1, TS)]
    te.wait_ge(sem.idn, 1)
    for step, t in enumerate([1, 2, 0, 3]):
        for x in range(TS):
            if x == 0 and t == 0:
                continue
            arrived(te, t, [x])
            mm = te.matmul(acc[x], T.ident[:], T.orecv[:, t, x, :], x > 0 and step == 0, t == 3)
            if t == 3:
                mm.then_inc(sem["zt%d" % x], 1)
    for x in range(TS):
        ac.wait_ge(sem["zt%d" % x], 1)
        ac.activation(T.ysb[:, x, :], acc[x], ActivationFunctionType.Copy).then_inc(sem.a3, 1)

    vh = list(range(TS, NW))
    b1, b2 = NB - 2, NB - 1
    for n in range(NG):
        ve.wait_ge(sem["rl%d" % n], 1)
    arrived(ve, 1, vh)
    arrived(ve, 2, vh)
    ve.tensor_tensor(T.sps[:, b1, TS:NH, :], T.orecv[:, 1, TS:NH, :], T.orecv[:, 2, TS:NH, :], AluOpType.add).then_inc(
        sem.a1b, 1)
    ve.wait_ge(sem.a1b, 1)
    arrived(ve, 0, vh)
    ve.tensor_tensor(T.sps[:, b2, TS:NH, :], T.sps[:, b1, TS:NH, :], T.orecv[:, 0, TS:NH, :], AluOpType.add).then_inc(
        sem.a2b, 1)
    ve.wait_ge(sem.a2b, 1)
    arrived(ve, 3, vh)
    ve.tensor_tensor(T.ysb[:, TS:NH, :], T.sps[:, b2, TS:NH, :], T.orecv[:, 3, TS:NH, :], AluOpType.add).then_inc(
        sem.a3, 1)

    g.sync.wait_ge(sem.a3, TS + 1)
    g.sync.dma_start(T.y[:], T.ysb[:]).then_inc(sem.st, 16)
    g.sync.wait_ge(sem.st, 16)
